import numpy as np
import ml_dtypes


def mxq(x, axis, fmt="e4m3"):
    dtype, down = {"e4m3": (ml_dtypes.float8_e4m3fn, 7), "e5m2": (ml_dtypes.float8_e5m2, 14)}[fmt]
    v = np.moveaxis(np.asarray(x, np.float32).astype(ml_dtypes.bfloat16).astype(np.float64), axis, -1)
    blocks = v.reshape(v.shape[:-1] + (-1, 32))
    amax = np.abs(blocks).max(-1, keepdims=True)
    byte = np.maximum(np.where(amax > 0, np.frexp(amax)[1] - 1 + 127, 0) - down, 1)
    scale = np.exp2(byte - 127.0)
    codes = (blocks / scale).astype(np.float32).astype(dtype).astype(np.float64)
    return np.moveaxis((codes * scale).reshape(v.shape), -1, axis)


WIDE = False


def mx_kscale(k):
    if not WIDE:
        return np.ones(k)
    levels = np.array([10, -10, 5, -5, 0])
    if k % 512:
        return np.exp2(np.random.permutation(np.resize(levels, k // 32))).repeat(32)
    a = np.empty((k // 512, 16))
    for p in range(k // 512):
        a[p, :8] = np.random.permutation(np.resize(levels, 8))
        for g in range(8):
            far = levels[np.abs(levels - a[p, g]) >= 10]
            a[p, g + 8] = far[np.random.randint(len(far))]
    return np.exp2(a.ravel()).repeat(32)


def f64(x):
    return np.asarray(x).astype(np.float64)


def striped(idx):
    return np.tile(np.asarray(idx).reshape(-1, 16).T, (8, 1)).astype(np.uint16)


def unstriped(offs):
    return offs[:16].T.reshape(-1).astype(np.int64)


E2M1 = np.array([0.0, 0.5, 1.0, 1.5, 2.0, 3.0, 4.0, 6.0, -0.0, -0.5, -1.0, -1.5, -2.0, -3.0, -4.0, -6.0])


def pack_weight(w, fmt):
    k, n = w.shape
    w = f64(np.asarray(w, np.float32).astype(ml_dtypes.bfloat16)).reshape(k // 32, 32, n)
    amax = np.abs(w).max(1)
    if fmt == "e4m3":
        byte = np.frexp(amax)[1] - 1 + 127 - 7
    else:
        mant, ex = np.frexp(amax / 6.0)
        byte = np.where(mant > 0.5, ex, ex - 1) + 127
    byte = np.clip(np.where(amax > 0, byte, 1), 1, 254)
    scaled = (w * np.exp2(127.0 - byte)[:, None, :]).reshape(k, n).astype(np.float32)
    by_word = np.ascontiguousarray(scaled.reshape(k // 512, 128, 4, n).transpose(0, 1, 3, 2))
    if fmt == "e4m3":
        words = by_word.astype(ml_dtypes.float8_e4m3fn).view(np.uint8)
    else:
        c = by_word.astype(ml_dtypes.float4_e2m1fn).view(np.uint8) & 0xF
        words = (c[..., 0::2] | (c[..., 1::2] << 4)).reshape(k // 512, 128, 2 * n)
    return np.ascontiguousarray(words), np.ascontiguousarray(byte.astype(np.uint8).reshape(k // 512, 16, n))


def unpack_weight(words, scales, fmt):
    g, _, n = scales.shape
    words = np.ascontiguousarray(words).reshape(g, 128, n, -1)
    if fmt == "e4m3":
        vals = words.view(ml_dtypes.float8_e4m3fn).astype(np.float64)
    else:
        nib = np.empty((g, 128, n, 4), np.uint8)
        nib[..., 0::2] = words & 0xF
        nib[..., 1::2] = words >> 4
        vals = E2M1[nib]
    vals = vals * np.repeat(np.exp2(scales.astype(np.float64) - 127.0), 8, axis=1)[..., None]
    return vals.transpose(0, 1, 3, 2).reshape(g * 512, n)


def softplus(v):
    return np.log(1.0 + np.exp(v))


def silu(v):
    return v / (1.0 + np.exp(-v))


def sigmoid(v):
    return 1.0 / (1.0 + np.exp(-v))


D, K, R, T, I, Q, G = 512, 512, 512, 2048, 512, 128, 32


def setup_inputs():
    n = np.random.standard_normal
    idx = np.random.permutation(T)[:I]
    fd = mx_kscale(D)
    fk = mx_kscale(K)
    fr = mx_kscale(R)
    keysp = pack_weight(n((D, T)) / fd[:, None], "e2m1")
    tabp = pack_weight(n((K, T)) / fk[:, None], "e2m1")
    return {
        "query": (n((D, Q)) * 0.9 / np.sqrt(D) * fd[:, None]).astype(np.float32),
        "keys_words": keysp[0],
        "keys_scales": keysp[1],
        "th": (np.random.uniform(-0.3, 0.6, (Q, 1))).astype(np.float32),
        "reserve": (np.random.uniform(50.0, 200.0, (Q, 1))).astype(np.float32),
        "tab_words": tabp[0],
        "tab_scales": tabp[1],
        "w1": (n((K, R)) * 1 / np.sqrt(K) * fk[:, None]).astype(np.float32),
        "gain": (np.random.uniform(0.7, 2.0, (R, 1))).astype(np.float32),
        "gout": (n((R, Q)) * 1 / np.sqrt(R) * fr[:, None]).astype(np.float32),
        "hsc": (np.random.uniform(0.7, 1.4, (R, 1)) / fr[:, None]).astype(np.float32),
        "old": (0.5 * n((Q, T))).astype(np.float32),
        "offs": striped(idx),
    }


def reference(query, keys_words, keys_scales, th, reserve, tab_words, tab_scales, w1, gain, gout, hsc, old, offs):
    idx = unstriped(offs)
    keysu = unpack_weight(keys_words, keys_scales, "e2m1")
    tabu = unpack_weight(tab_words, tab_scales, "e2m1")
    queryq = mxq(f64(query), 0, "e4m3")
    keysidxg = keysu[:, idx]
    a = queryq.T @ keysidxg
    p = softplus(a - f64(th))
    z = np.sum(p, axis=1, keepdims=True) + f64(reserve)
    w1q = mxq(f64(w1), 0, "e4m3")
    tabidxg = tabu[:, idx]
    zh = w1q.T @ tabidxg
    mz = np.sqrt(np.square(zh).reshape(R, G, I // G).mean(axis=2) + 0.1)
    mzr = np.repeat(mz, I // G, axis=1)
    hv = silu(zh / mzr * f64(gain))
    hs1 = hv * f64(hsc)
    goutq = mxq(f64(gout), 0, "e4m3")
    hs1q = mxq(hs1, 0, "e4m3")
    c0 = goutq.T @ hs1q
    dz = np.sum(c0 * p / np.square(z) * (-1.0), axis=1, keepdims=True)
    dp = c0 / z + dz
    da = dp * sigmoid(a - f64(th))
    gs = da * 512.0
    gf = np.zeros((Q, T))
    gf[:, idx] = gs
    y = f64(old) + gf
    return y

@@ -1,0 +1,239 @@
+from contextlib import ExitStack
+
+import concourse.mybir as mybir
+from concourse.masks import make_identity
+
+D, K, R, T, I, Q, G = 512, 512, 512, 2048, 512, 128, 32
+FLOPS = 2 * I * (D * Q + K * R + R * Q)
+
+F32 = mybir.dt.float32
+BF16 = mybir.dt.bfloat16
+I32 = mybir.dt.int32
+U32 = mybir.dt.uint32
+U16 = mybir.dt.uint16
+U8 = mybir.dt.uint8
+FP8X4 = mybir.dt.float8_e4m3fn_x4
+FP4X4 = mybir.dt.float4_e2m1fn_x4
+ACT = mybir.ActivationFunctionType
+ALU = mybir.AluOpType
+
+P = 128
+PACK = 4
+PAGE = I // G
+CH = 128
+NCH = I // CH
+RUN = PAGE // NCH
+OUT_EDGES = (0, 512, 1024, 1536, 1792, 2048)
+
+
+def tile_attend_blrscaled_capped_kernel(tc, query, keys_words, keys_scales, th, reserve, tab_words, tab_scales,
+                                         w1, gain, gout, hsc, old, offs, out):
+    nc = tc.nc
+    with ExitStack() as ctx:
+        sb = ctx.enter_context(tc.tile_pool(name="sb", bufs=1))
+        ps = ctx.enter_context(tc.psum_pool(name="ps", bufs=1))
+
+        def tile(name, shape, dtype, tag=None):
+            return sb.tile(shape, dtype, name=name, tag=tag or name, align_bytes=64)
+
+        offsets = tile("offsets", [P, I // 16], U16)
+        nc.sync.dma_start(offsets[:], offs)
+
+        def load_scales(name, src, clear, queue):
+            plane = tile(name, [P, T], U8)
+            clear.memset(plane[:].bitcast(I32), 0)
+            for quad in range(4):
+                queue.dma_start(plane[32 * quad:32 * quad + 4, :].bitcast(I32),
+                                src[0, 4 * quad:4 * quad + 4, :].bitcast(I32))
+            return plane
+
+        def load_words(name, src, tag):
+            words = tile(name, [P, T], U16, tag)
+            nc.sync.dma_start(words[:].bitcast(I32), src[0].bitcast(I32))
+            return words
+
+        tab_sc = load_scales("tab_sc", tab_scales, nc.gpsimd, nc.scalar)
+        warm_in = tile("warm_in", [P, 1], F32)
+        warm_out = tile("warm_out", [P, 1], F32)
+        nc.gpsimd.memset(warm_in[:], 1.0)
+        nc.scalar.activation(warm_out[:], warm_in[:], ACT.Abs_reciprocal_sqrt)
+        tab_w = load_words("tab_w", tab_words, "words")
+        w1_rows = w1.rearrange("(p j) c -> p j c", j=PACK)
+        w1_raw = []
+        for h in range(2):
+            raw = tile("w1_raw%d" % h, [P, PACK, 256], F32)
+            nc.sync.dma_start(raw[:], w1_rows[:, :, 256 * h:256 * (h + 1)])
+            w1_raw.append(raw)
+
+        window = tile("window", [P, T], F32)
+        nc.vector.memset(window[:, :T // 2], 0.0)
+        nc.gpsimd.memset(window[:, T // 2:], 0.0)
+        keys_sc = load_scales("keys_sc", keys_scales, nc.vector, nc.sync)
+        ident = tile("ident", [P, P], F32)
+        make_identity(nc, ident[:])
+        gain_sb = tile("gain_sb", [P, PACK], F32)
+        nc.gpsimd.dma_start(gain_sb[:], gain.rearrange("(p j) o -> p (j o)", j=PACK))
+        th_sb = tile("th_sb", [P, 1], F32)
+        nc.gpsimd.dma_start(th_sb[:], th)
+        hsc_sb = tile("hsc_sb", [P, PACK], F32)
+        nc.gpsimd.dma_start(hsc_sb[:], hsc.rearrange("(p j) o -> p (j o)", j=PACK))
+        res_sb = tile("res_sb", [P, 1], F32)
+        nc.gpsimd.dma_start(res_sb[:], reserve)
+
+        def gather(name, src, dtype):
+            dst = tile(name, [P, I], dtype)
+            nc.vector.tensor_copy(dst[:], src[:].indirect(offsets[:]))
+            return dst
+
+        def deal(name, src, dtype):
+            dst = tile(name, [P, I], dtype)
+            nc.vector.tensor_copy(dst[:].bitcast(I32).rearrange("p (h g w) -> p h g w", h=NCH, g=G),
+                                  src[:].bitcast(I32).rearrange("p (g h w) -> p h g w", h=NCH, g=G))
+            return dst
+
+        tab_gw = gather("tab_gw", tab_w, U16)
+        keys_w = load_words("keys_w", keys_words, "words")
+        tab_gs = gather("tab_gs", tab_sc, U8)
+        tab_dw = deal("tab_dw", tab_gw, U16)
+        tab_ds = deal("tab_ds", tab_gs, U8)
+
+        w1_bf = tile("w1_bf", [P, PACK, P, PACK], BF16)
+        for c in range(4):
+            src = w1_raw[c // 2][:, :, 128 * (c % 2):128 * (c % 2 + 1)].rearrange("p j (m t) -> p m j t", t=PACK)
+            dst = w1_bf[:, :, 32 * c:32 * (c + 1), :].rearrange("p t m j -> p m j t")
+            if c >= 3:
+                nc.vector.tensor_copy(dst, src)
+            else:
+                nc.scalar.copy(dst, src)
+        q_raw = tile("q_raw", [P, PACK, Q], F32, tag="w1_raw0")
+        nc.sync.dma_start(q_raw[:], query.rearrange("(p j) c -> p j c", j=PACK))
+        g_raw = tile("g_raw", [P, PACK, Q], F32, tag="w1_raw1")
+        nc.sync.dma_start(g_raw[:], gout.rearrange("(p j) c -> p j c", j=PACK))
+        w1_codes = tile("w1_codes", [P, R], U32)
+        w1_scales = tile("w1_scales", [P, R], U8)
+        for t in range(PACK):
+            cols = slice(P * t, P * (t + 1))
+            nc.vector.quantize_mx(out=w1_codes[:, cols].bitcast(FP8X4), scales=w1_scales[:, cols],
+                                  in_=w1_bf[:, t].rearrange("p m j -> p (m j)"))
+
+        zh = []
+        for h in range(NCH):
+            bank = ps.tile([P, PACK, CH], F32, name="zh%d" % h)
+            slots = slice(CH * h, CH * (h + 1))
+            for t in range(PACK):
+                cols = slice(P * t, P * (t + 1))
+                nc.tensor.matmul_mx(out=bank[:, t, :], lhsT=w1_codes[:, cols].bitcast(FP8X4),
+                                    lhsT_scale=w1_scales[:, cols], rhs=tab_dw[:, slots].bitcast(FP4X4),
+                                    rhs_scale=tab_ds[:, slots], start=True, stop=True)
+            zh.append(bank)
+
+        sq = tile("sq", [P, NCH, RUN, G * PACK], F32)
+        ssq_t = ps.tile([P, P], F32, name="ssq_t")
+        for h in range(NCH):
+            nc.scalar.activation(sq[:, h].rearrange("p j (g t) -> p j g t", t=PACK),
+                                 zh[h][:].rearrange("p t (g j) -> p j g t", j=RUN), ACT.Square)
+            for j in range(RUN):
+                nc.tensor.matmul(ssq_t[:], sq[:, h, j, :], ident[:], is_transpose=True,
+                                 start=(h == 0 and j == 0), stop=(h == NCH - 1 and j == RUN - 1))
+        inv_t = tile("inv_t", [P, P], F32)
+        nc.scalar.activation(inv_t[:], ssq_t[:], ACT.Abs_reciprocal_sqrt, bias=0.1, scale=1.0 / PAGE)
+        inv = ps.tile([P, G, PACK], F32, name="inv")
+        nc.tensor.transpose(inv[:].rearrange("p g t -> p (g t)"), inv_t[:], ident[:])
+        old_sb = tile("old_sb", [P, T], F32, tag="sq")
+        nc.sync.dma_start(old_sb[:], old)
+
+        def quantise_cols(name, raw, copy):
+            bf = tile(name + "_bf", [P, Q, PACK], BF16)
+            copy(bf[:].rearrange("p (c i) j -> p c j i", i=4), raw[:].rearrange("p j (c i) -> p c j i", i=4))
+            codes = tile(name + "_codes", [P, Q], U32)
+            scales = tile(name + "_scales", [P, Q], U8)
+            nc.vector.quantize_mx(out=codes[:].bitcast(FP8X4), scales=scales[:],
+                                  in_=bf[:].rearrange("p c j -> p (c j)"))
+            return codes, scales
+
+        keys_gw = gather("keys_gw", keys_w, U16)
+        keys_gs = gather("keys_gs", keys_sc, U8)
+        q_codes, q_scales = quantise_cols("q", q_raw, nc.vector.tensor_copy)
+        score = ps.tile([P, I], F32, name="score")
+        nc.tensor.matmul_mx(out=score[:], lhsT=q_codes[:].bitcast(FP8X4), lhsT_scale=q_scales[:],
+                            rhs=keys_gw[:].bitcast(FP4X4), rhs_scale=keys_gs[:], start=True, stop=True)
+        g_codes, g_scales = quantise_cols("g", g_raw, nc.vector.tensor_copy)
+        fac = tile("fac", [P, G, PACK], F32)
+        nc.vector.tensor_tensor(fac[:], inv[:], gain_sb[:].unsqueeze(1).to_broadcast([P, G, PACK]), ALU.mult)
+        neg_th = tile("neg_th", [P, 1], F32)
+        nc.gpsimd.tensor_scalar(neg_th[:], th_sb[:], -1.0, 0.0, ALU.mult, ALU.add)
+        neg_half_th = tile("neg_half_th", [P, 1], F32)
+        nc.gpsimd.tensor_scalar(neg_half_th[:], th_sb[:], -0.5, 0.0, ALU.mult, ALU.add)
+
+        c0 = ps.tile([P, I], F32, name="c0")
+        u = [tile("u%d" % h, [P, CH * PACK], F32) for h in range(NCH)]
+        hv = [tile("hv%d" % h, [P, CH, PACK], F32) for h in range(NCH)]
+        for h in range(NCH):
+            nc.vector.tensor_tensor(
+                u[h][:].rearrange("p (g j t) -> p g j t", j=RUN, t=PACK),
+                zh[h][:].rearrange("p t (g j) -> p g j t", j=RUN),
+                fac[:].unsqueeze(2).to_broadcast([P, G, RUN, PACK]), ALU.mult)
+        relu = u[2]
+        sum_relu = tile("sum_relu", [P, 1], F32)
+        tanh = u[1]
+        logs = u[NCH - 1]
+        abs_tanh = tile("abs_tanh", [P, I], F32)
+        score_dealt = score[:].rearrange("p (g h j) -> p h g j", h=NCH, j=RUN)
+
+        def dealt(ap):
+            return ap.rearrange("p (h g j) -> p h g j", h=NCH, j=RUN)
+
+        def listed(ap):
+            return ap.rearrange("p (h g j) -> p g h j", h=NCH, j=RUN)
+
+        def by_page(ap):
+            return ap.rearrange("p (g h j) -> p g h j", h=NCH, j=RUN)
+
+        for h in range(NCH):
+            nc.scalar.activation(hv[h][:].rearrange("p i t -> p (i t)"), u[h][:], ACT.Silu)
+            if h == 1:
+                nc.scalar.activation(dealt(tanh[:]), score_dealt, ACT.Tanh, bias=neg_half_th[:], scale=0.5)
+            if h == 2:
+                nc.scalar.activation(dealt(relu[:]), score_dealt, ACT.Relu, bias=neg_th[:], accum_out=sum_relu[:])
+        for h in range(NCH):
+            hs = tile("hs%d" % h, [P, CH, PACK], BF16)
+            eng = nc.gpsimd if h in () else nc.vector
+            eng.tensor_tensor(hs[:], hv[h][:], hsc_sb[:].unsqueeze(1).to_broadcast([P, CH, PACK]), ALU.mult)
+            if h == 1:
+                nc.vector.scalar_tensor_tensor(abs_tanh[:], tanh[:], -1.0, tanh[:], ALU.mult, ALU.max)
+            codes = tile("hs_codes%d" % h, [P, CH], U32)
+            scales = tile("hs_scales%d" % h, [P, CH], U8)
+            nc.vector.quantize_mx(out=codes[:].bitcast(FP8X4), scales=scales[:],
+                                  in_=hs[:].rearrange("p i t -> p (i t)"))
+            nc.tensor.matmul_mx(out=c0[:, CH * h:CH * (h + 1)], lhsT=g_codes[:].bitcast(FP8X4),
+                                lhsT_scale=g_scales[:], rhs=codes[:].bitcast(FP8X4), rhs_scale=scales[:],
+                                start=True, stop=True)
+
+        base = tile("base", [P, 1], F32)
+        nc.gpsimd.tensor_tensor(base[:], sum_relu[:], res_sb[:], ALU.add)
+        sum_log = tile("sum_log", [P, 1], F32)
+        nc.scalar.activation(logs[:], abs_tanh[:], ACT.Ln, bias=0.5, scale=0.5, accum_out=sum_log[:])
+        sig = abs_tanh
+        nc.scalar.activation(by_page(sig[:]), listed(tanh[:]), ACT.Identity, bias=256.0, scale=256.0)
+
+        junk = tile("junk", [P, I], F32)
+        dot_relu = tile("dot_relu", [P, 1], F32)
+        nc.vector.scalar_tensor_tensor(junk[:], c0[:], 1.0, relu[:], ALU.mult, ALU.mult, accum_out=dot_relu[:])
+        z = tile("z", [P, 1], F32)
+        nc.vector.tensor_tensor(z[:], base[:], sum_log[:], ALU.subtract)
+        junk2 = tile("junk2", [P, I], F32)
+        dot_log = tile("dot_log", [P, 1], F32)
+        nc.vector.scalar_tensor_tensor(junk2[:], c0[:], 1.0, logs[:], ALU.mult, ALU.mult, accum_out=dot_log[:])
+        rz = tile("rz", [P, 1], F32)
+        nc.vector.reciprocal(rz[:], z[:])
+        shift = tile("shift", [P, 1], F32)
+        nc.vector.tensor_scalar(shift[:], dot_log[:], dot_relu[:], rz[:], ALU.subtract, ALU.mult)
+        dp = tile("dp", [P, I], F32)
+        nc.vector.tensor_scalar(by_page(dp[:]), listed(c0[:]), shift[:], rz[:], ALU.add, ALU.mult)
+        nc.vector.tensor_tensor(window[:].indirect(offsets[:]), dp[:], sig[:], ALU.mult)
+
+        for c in range(len(OUT_EDGES) - 1):
+            cols = slice(OUT_EDGES[c], OUT_EDGES[c + 1])
+            res = tile("res%d" % c, [P, OUT_EDGES[c + 1] - OUT_EDGES[c]], F32)
+            nc.vector.tensor_tensor(res[:], window[:, cols], old_sb[:, cols], ALU.add)
+            (nc.sync if c % 2 == 0 else nc.scalar).dma_start(out[:, cols], res[:])

@@ -23,7 +23,7 @@ PAGE = I // G
 CH = 128
 NCH = I // CH
 RUN = PAGE // NCH
-OUT_EDGES = (0, 512, 1024, 1536, 1792, 2048)
+OUT_EDGES = (0, 256, 768, 1280, 1792, 2048)
 
 
 def tile_attend_blrscaled_capped_kernel(tc, query, keys_words, keys_scales, th, reserve, tab_words, tab_scales,
@@ -53,10 +53,6 @@ def tile_attend_blrscaled_capped_kernel(tc, query, keys_words, keys_scales, th, 
             return words
 
         tab_sc = load_scales("tab_sc", tab_scales, nc.gpsimd, nc.scalar)
-        warm_in = tile("warm_in", [P, 1], F32)
-        warm_out = tile("warm_out", [P, 1], F32)
-        nc.gpsimd.memset(warm_in[:], 1.0)
-        nc.scalar.activation(warm_out[:], warm_in[:], ACT.Abs_reciprocal_sqrt)
         tab_w = load_words("tab_w", tab_words, "words")
         w1_rows = w1.rearrange("(p j) c -> p j c", j=PACK)
         w1_raw = []
@@ -64,6 +60,8 @@ def tile_attend_blrscaled_capped_kernel(tc, query, keys_words, keys_scales, th, 
             raw = tile("w1_raw%d" % h, [P, PACK, 256], F32)
             nc.sync.dma_start(raw[:], w1_rows[:, :, 256 * h:256 * (h + 1)])
             w1_raw.append(raw)
+        warm_out = tile("warm_out", [P, 1], F32)
+        nc.scalar.activation(warm_out[:], w1_raw[0][:, 0, 0:1], ACT.Abs_reciprocal_sqrt, bias=1.0, scale=0.0)
 
         window = tile("window", [P, T], F32)
         nc.vector.memset(window[:, :T // 2], 0.0)
@@ -71,17 +69,9 @@ def tile_attend_blrscaled_capped_kernel(tc, query, keys_words, keys_scales, th, 
         keys_sc = load_scales("keys_sc", keys_scales, nc.vector, nc.sync)
         ident = tile("ident", [P, P], F32)
         make_identity(nc, ident[:])
-        gain_sb = tile("gain_sb", [P, PACK], F32)
-        nc.gpsimd.dma_start(gain_sb[:], gain.rearrange("(p j) o -> p (j o)", j=PACK))
-        th_sb = tile("th_sb", [P, 1], F32)
-        nc.gpsimd.dma_start(th_sb[:], th)
-        hsc_sb = tile("hsc_sb", [P, PACK], F32)
-        nc.gpsimd.dma_start(hsc_sb[:], hsc.rearrange("(p j) o -> p (j o)", j=PACK))
-        res_sb = tile("res_sb", [P, 1], F32)
-        nc.gpsimd.dma_start(res_sb[:], reserve)
 
-        def gather(name, src, dtype):
-            dst = tile(name, [P, I], dtype)
+        def gather(name, src, dtype, tag=None):
+            dst = tile(name, [P, I], dtype, tag)
             nc.vector.tensor_copy(dst[:], src[:].indirect(offsets[:]))
             return dst
 
@@ -116,6 +106,13 @@ def tile_attend_blrscaled_capped_kernel(tc, query, keys_words, keys_scales, th, 
             nc.vector.quantize_mx(out=w1_codes[:, cols].bitcast(FP8X4), scales=w1_scales[:, cols],
                                   in_=w1_bf[:, t].rearrange("p m j -> p (m j)"))
 
+        gain_sb = tile("gain_sb", [P, PACK], F32, tag="tab_sc")
+        nc.sync.dma_start(gain_sb[:], gain.rearrange("(p j) o -> p (j o)", j=PACK))
+        th_sb = tile("th_sb", [P, 1], F32, tag="tab_gw")
+        nc.sync.dma_start(th_sb[:], th)
+        hsc_sb = tile("hsc_sb", [P, PACK], F32, tag="tab_gs")
+        nc.sync.dma_start(hsc_sb[:], hsc.rearrange("(p j) o -> p (j o)", j=PACK))
+
         zh = []
         for h in range(NCH):
             bank = ps.tile([P, PACK, CH], F32, name="zh%d" % h)
@@ -127,23 +124,23 @@ def tile_attend_blrscaled_capped_kernel(tc, query, keys_words, keys_scales, th, 
                                     rhs_scale=tab_ds[:, slots], start=True, stop=True)
             zh.append(bank)
 
-        sq = tile("sq", [P, NCH, RUN, G * PACK], F32)
-        ssq_t = ps.tile([P, P], F32, name="ssq_t")
+        sq_pe = tile("sq_pe", [P, NCH, RUN, G * PACK], F32)
+        ssq_t = ps.tile([P, P], F32, name="ssq_t", tag="shared")
         for h in range(NCH):
-            nc.scalar.activation(sq[:, h].rearrange("p j (g t) -> p j g t", t=PACK),
+            nc.scalar.activation(sq_pe[:, h].rearrange("p j (g t) -> p j g t", t=PACK),
                                  zh[h][:].rearrange("p t (g j) -> p j g t", j=RUN), ACT.Square)
             for j in range(RUN):
-                nc.tensor.matmul(ssq_t[:], sq[:, h, j, :], ident[:], is_transpose=True,
+                nc.tensor.matmul(ssq_t[:], sq_pe[:, h, j, :], ident[:], is_transpose=True,
                                  start=(h == 0 and j == 0), stop=(h == NCH - 1 and j == RUN - 1))
         inv_t = tile("inv_t", [P, P], F32)
         nc.scalar.activation(inv_t[:], ssq_t[:], ACT.Abs_reciprocal_sqrt, bias=0.1, scale=1.0 / PAGE)
         inv = ps.tile([P, G, PACK], F32, name="inv")
         nc.tensor.transpose(inv[:].rearrange("p g t -> p (g t)"), inv_t[:], ident[:])
-        old_sb = tile("old_sb", [P, T], F32, tag="sq")
+        old_sb = tile("old_sb", [P, T], F32, tag="sq_pe")
         nc.sync.dma_start(old_sb[:], old)
 
-        def quantise_cols(name, raw, copy):
-            bf = tile(name + "_bf", [P, Q, PACK], BF16)
+        def quantise_cols(name, raw, copy, tag):
+            bf = tile(name + "_bf", [P, Q, PACK], BF16, tag)
             copy(bf[:].rearrange("p (c i) j -> p c j i", i=4), raw[:].rearrange("p j (c i) -> p c j i", i=4))
             codes = tile(name + "_codes", [P, Q], U32)
             scales = tile(name + "_scales", [P, Q], U8)
@@ -153,11 +150,12 @@ def tile_attend_blrscaled_capped_kernel(tc, query, keys_words, keys_scales, th, 
 
         keys_gw = gather("keys_gw", keys_w, U16)
         keys_gs = gather("keys_gs", keys_sc, U8)
-        q_codes, q_scales = quantise_cols("q", q_raw, nc.vector.tensor_copy)
-        score = ps.tile([P, I], F32, name="score")
+        res_sb = tile("res_sb", [P, 1], F32, tag="keys_sc")
+        nc.sync.dma_start(res_sb[:], reserve)
+        q_codes, q_scales = quantise_cols("q", q_raw, nc.vector.tensor_copy, "q_bf")
+        score = ps.tile([P, I], F32, name="score", tag="shared")
         nc.tensor.matmul_mx(out=score[:], lhsT=q_codes[:].bitcast(FP8X4), lhsT_scale=q_scales[:],
                             rhs=keys_gw[:].bitcast(FP4X4), rhs_scale=keys_gs[:], start=True, stop=True)
-        g_codes, g_scales = quantise_cols("g", g_raw, nc.vector.tensor_copy)
         fac = tile("fac", [P, G, PACK], F32)
         nc.vector.tensor_tensor(fac[:], inv[:], gain_sb[:].unsqueeze(1).to_broadcast([P, G, PACK]), ALU.mult)
         neg_th = tile("neg_th", [P, 1], F32)
@@ -173,10 +171,11 @@ def tile_attend_blrscaled_capped_kernel(tc, query, keys_words, keys_scales, th, 
                 u[h][:].rearrange("p (g j t) -> p g j t", j=RUN, t=PACK),
                 zh[h][:].rearrange("p t (g j) -> p g j t", j=RUN),
                 fac[:].unsqueeze(2).to_broadcast([P, G, RUN, PACK]), ALU.mult)
-        relu = u[2]
+        g_codes, g_scales = quantise_cols("g", g_raw, nc.vector.tensor_copy, "g_bf")
+        relu = u[2][:]
         sum_relu = tile("sum_relu", [P, 1], F32)
-        tanh = u[1]
-        logs = u[NCH - 1]
+        tanh = u[3]
+        logs = u[1]
         abs_tanh = tile("abs_tanh", [P, I], F32)
         score_dealt = score[:].rearrange("p (g h j) -> p h g j", h=NCH, j=RUN)
 
@@ -191,16 +190,13 @@ def tile_attend_blrscaled_capped_kernel(tc, query, keys_words, keys_scales, th, 
 
         for h in range(NCH):
             nc.scalar.activation(hv[h][:].rearrange("p i t -> p (i t)"), u[h][:], ACT.Silu)
-            if h == 1:
+            if h == 3:
                 nc.scalar.activation(dealt(tanh[:]), score_dealt, ACT.Tanh, bias=neg_half_th[:], scale=0.5)
-            if h == 2:
-                nc.scalar.activation(dealt(relu[:]), score_dealt, ACT.Relu, bias=neg_th[:], accum_out=sum_relu[:])
+        nc.scalar.activation(dealt(relu), score_dealt, ACT.Relu, bias=neg_th[:], accum_out=sum_relu[:])
         for h in range(NCH):
             hs = tile("hs%d" % h, [P, CH, PACK], BF16)
-            eng = nc.gpsimd if h in () else nc.vector
+            eng = nc.gpsimd if h in (0,) else nc.vector
             eng.tensor_tensor(hs[:], hv[h][:], hsc_sb[:].unsqueeze(1).to_broadcast([P, CH, PACK]), ALU.mult)
-            if h == 1:
-                nc.vector.scalar_tensor_tensor(abs_tanh[:], tanh[:], -1.0, tanh[:], ALU.mult, ALU.max)
             codes = tile("hs_codes%d" % h, [P, CH], U32)
             scales = tile("hs_scales%d" % h, [P, CH], U8)
             nc.vector.quantize_mx(out=codes[:].bitcast(FP8X4), scales=scales[:],
@@ -209,18 +205,19 @@ def tile_attend_blrscaled_capped_kernel(tc, query, keys_words, keys_scales, th, 
                                 lhsT_scale=g_scales[:], rhs=codes[:].bitcast(FP8X4), rhs_scale=scales[:],
                                 start=True, stop=True)
 
+        nc.vector.scalar_tensor_tensor(abs_tanh[:], tanh[:], -1.0, tanh[:], ALU.mult, ALU.max)
         base = tile("base", [P, 1], F32)
         nc.gpsimd.tensor_tensor(base[:], sum_relu[:], res_sb[:], ALU.add)
         sum_log = tile("sum_log", [P, 1], F32)
         nc.scalar.activation(logs[:], abs_tanh[:], ACT.Ln, bias=0.5, scale=0.5, accum_out=sum_log[:])
+        z = tile("z", [P, 1], F32)
+        nc.scalar.activation(z[:], sum_log[:], ACT.Identity, bias=base[:], scale=-1.0)
         sig = abs_tanh
         nc.scalar.activation(by_page(sig[:]), listed(tanh[:]), ACT.Identity, bias=256.0, scale=256.0)
 
         junk = tile("junk", [P, I], F32)
         dot_relu = tile("dot_relu", [P, 1], F32)
-        nc.vector.scalar_tensor_tensor(junk[:], c0[:], 1.0, relu[:], ALU.mult, ALU.mult, accum_out=dot_relu[:])
-        z = tile("z", [P, 1], F32)
-        nc.vector.tensor_tensor(z[:], base[:], sum_log[:], ALU.subtract)
+        nc.vector.scalar_tensor_tensor(junk[:], c0[:], 1.0, relu, ALU.mult, ALU.mult, accum_out=dot_relu[:])
         junk2 = tile("junk2", [P, I], F32)
         dot_log = tile("dot_log", [P, 1], F32)
         nc.vector.scalar_tensor_tensor(junk2[:], c0[:], 1.0, logs[:], ALU.mult, ALU.mult, accum_out=dot_log[:])

@@ -52,7 +52,7 @@ def tile_attend_blrscaled_capped_kernel(tc, query, keys_words, keys_scales, th, 
             nc.sync.dma_start(words[:].bitcast(I32), src[0].bitcast(I32))
             return words
 
-        tab_sc = load_scales("tab_sc", tab_scales, nc.gpsimd, nc.scalar)
+        tab_sc = load_scales("tab_sc", tab_scales, nc.vector, nc.scalar)
         tab_w = load_words("tab_w", tab_words, "words")
         w1_rows = w1.rearrange("(p j) c -> p j c", j=PACK)
         w1_raw = []
@@ -64,9 +64,8 @@ def tile_attend_blrscaled_capped_kernel(tc, query, keys_words, keys_scales, th, 
         nc.scalar.activation(warm_out[:], w1_raw[0][:, 0, 0:1], ACT.Abs_reciprocal_sqrt, bias=1.0, scale=0.0)
 
         window = tile("window", [P, T], F32)
-        nc.vector.memset(window[:, :T // 2], 0.0)
-        nc.gpsimd.memset(window[:, T // 2:], 0.0)
         keys_sc = load_scales("keys_sc", keys_scales, nc.vector, nc.sync)
+        nc.vector.memset(window[:], 0.0)
         ident = tile("ident", [P, P], F32)
         make_identity(nc, ident[:])
 
@@ -89,8 +88,8 @@ def tile_attend_blrscaled_capped_kernel(tc, query, keys_words, keys_scales, th, 
 
         w1_bf = tile("w1_bf", [P, PACK, P, PACK], BF16)
         for c in range(4):
-            src = w1_raw[c // 2][:, :, 128 * (c % 2):128 * (c % 2 + 1)].rearrange("p j (m t) -> p m j t", t=PACK)
-            dst = w1_bf[:, :, 32 * c:32 * (c + 1), :].rearrange("p t m j -> p m j t")
+            src = w1_raw[c // 2][:, :, 128 * (c % 2):128 * (c % 2 + 1)].rearrange("p j (m t) -> p t m j", t=PACK)
+            dst = w1_bf[:, :, 32 * c:32 * (c + 1), :]
             if c >= 3:
                 nc.vector.tensor_copy(dst, src)
             else:
@@ -159,9 +158,9 @@ def tile_attend_blrscaled_capped_kernel(tc, query, keys_words, keys_scales, th, 
         fac = tile("fac", [P, G, PACK], F32)
         nc.vector.tensor_tensor(fac[:], inv[:], gain_sb[:].unsqueeze(1).to_broadcast([P, G, PACK]), ALU.mult)
         neg_th = tile("neg_th", [P, 1], F32)
-        nc.gpsimd.tensor_scalar(neg_th[:], th_sb[:], -1.0, 0.0, ALU.mult, ALU.add)
+        nc.vector.tensor_scalar(neg_th[:], th_sb[:], -1.0, None, ALU.mult)
         neg_half_th = tile("neg_half_th", [P, 1], F32)
-        nc.gpsimd.tensor_scalar(neg_half_th[:], th_sb[:], -0.5, 0.0, ALU.mult, ALU.add)
+        nc.vector.tensor_scalar(neg_half_th[:], th_sb[:], -0.5, None, ALU.mult)
 
         c0 = ps.tile([P, I], F32, name="c0")
         u = [tile("u%d" % h, [P, CH * PACK], F32) for h in range(NCH)]
@@ -195,8 +194,7 @@ def tile_attend_blrscaled_capped_kernel(tc, query, keys_words, keys_scales, th, 
         nc.scalar.activation(dealt(relu), score_dealt, ACT.Relu, bias=neg_th[:], accum_out=sum_relu[:])
         for h in range(NCH):
             hs = tile("hs%d" % h, [P, CH, PACK], BF16)
-            eng = nc.gpsimd if h in (0,) else nc.vector
-            eng.tensor_tensor(hs[:], hv[h][:], hsc_sb[:].unsqueeze(1).to_broadcast([P, CH, PACK]), ALU.mult)
+            nc.vector.tensor_tensor(hs[:], hv[h][:], hsc_sb[:].unsqueeze(1).to_broadcast([P, CH, PACK]), ALU.mult)
             codes = tile("hs_codes%d" % h, [P, CH], U32)
             scales = tile("hs_scales%d" % h, [P, CH], U8)
             nc.vector.quantize_mx(out=codes[:].bitcast(FP8X4), scales=scales[:],
@@ -207,7 +205,7 @@ def tile_attend_blrscaled_capped_kernel(tc, query, keys_words, keys_scales, th, 
 
         nc.vector.scalar_tensor_tensor(abs_tanh[:], tanh[:], -1.0, tanh[:], ALU.mult, ALU.max)
         base = tile("base", [P, 1], F32)
-        nc.gpsimd.tensor_tensor(base[:], sum_relu[:], res_sb[:], ALU.add)
+        nc.scalar.activation(base[:], sum_relu[:], ACT.Identity, bias=res_sb[:])
         sum_log = tile("sum_log", [P, 1], F32)
         nc.scalar.activation(logs[:], abs_tanh[:], ACT.Ln, bias=0.5, scale=0.5, accum_out=sum_log[:])
         z = tile("z", [P, 1], F32)

@@ -20,10 +20,28 @@ ALU = mybir.AluOpType
 P = 128
 PACK = 4
 PAGE = I // G
-CH = 128
-NCH = I // CH
-RUN = PAGE // NCH
+QUARTERS = 4
+RUN = PAGE // QUARTERS
+BANK_SLOTS = G * RUN
+W1_LOADS = 2
+W1_COPIES = 4
 OUT_EDGES = (0, 256, 768, 1280, 1792, 2048)
+
+
+def dealt_from_listed(ap):
+    return ap.rearrange("p (g h j) -> p h g j", h=QUARTERS, j=RUN)
+
+
+def listed_from_dealt(ap):
+    return ap.rearrange("p (h g j) -> p g h j", h=QUARTERS, j=RUN)
+
+
+def as_dealt(ap):
+    return ap.rearrange("p (h g j) -> p h g j", h=QUARTERS, j=RUN)
+
+
+def as_listed(ap):
+    return ap.rearrange("p (g h j) -> p g h j", h=QUARTERS, j=RUN)
 
 
 def tile_attend_blrscaled_capped_kernel(tc, query, keys_words, keys_scales, th, reserve, tab_words, tab_scales,
@@ -36,86 +54,102 @@ def tile_attend_blrscaled_capped_kernel(tc, query, keys_words, keys_scales, th, 
         def tile(name, shape, dtype, tag=None):
             return sb.tile(shape, dtype, name=name, tag=tag or name, align_bytes=64)
 
-        offsets = tile("offsets", [P, I // 16], U16)
-        nc.sync.dma_start(offsets[:], offs)
-
-        def load_scales(name, src, clear, queue):
+        def load_scales(name, src, clear):
             plane = tile(name, [P, T], U8)
             clear.memset(plane[:].bitcast(I32), 0)
             for quad in range(4):
-                queue.dma_start(plane[32 * quad:32 * quad + 4, :].bitcast(I32),
-                                src[0, 4 * quad:4 * quad + 4, :].bitcast(I32))
+                nc.sync.dma_start(plane[32 * quad:32 * quad + 4, :].bitcast(I32),
+                                  src[0, 4 * quad:4 * quad + 4, :].bitcast(I32))
             return plane
 
-        def load_words(name, src, tag):
-            words = tile(name, [P, T], U16, tag)
+        def load_words(name, src):
+            words = tile(name, [P, T], U16, "words")
             nc.sync.dma_start(words[:].bitcast(I32), src[0].bitcast(I32))
             return words
 
-        tab_sc = load_scales("tab_sc", tab_scales, nc.vector, nc.scalar)
-        tab_w = load_words("tab_w", tab_words, "words")
-        w1_rows = w1.rearrange("(p j) c -> p j c", j=PACK)
-        w1_raw = []
-        for h in range(2):
-            raw = tile("w1_raw%d" % h, [P, PACK, 256], F32)
-            nc.sync.dma_start(raw[:], w1_rows[:, :, 256 * h:256 * (h + 1)])
-            w1_raw.append(raw)
-        warm_out = tile("warm_out", [P, 1], F32)
-        nc.scalar.activation(warm_out[:], w1_raw[0][:, 0, 0:1], ACT.Abs_reciprocal_sqrt, bias=1.0, scale=0.0)
-
-        window = tile("window", [P, T], F32)
-        keys_sc = load_scales("keys_sc", keys_scales, nc.vector, nc.sync)
-        nc.vector.memset(window[:], 0.0)
-        ident = tile("ident", [P, P], F32)
-        make_identity(nc, ident[:])
-
-        def gather(name, src, dtype, tag=None):
-            dst = tile(name, [P, I], dtype, tag)
+        def gather(name, src, dtype):
+            dst = tile(name, [P, I], dtype)
             nc.vector.tensor_copy(dst[:], src[:].indirect(offsets[:]))
             return dst
 
         def deal(name, src, dtype):
             dst = tile(name, [P, I], dtype)
-            nc.vector.tensor_copy(dst[:].bitcast(I32).rearrange("p (h g w) -> p h g w", h=NCH, g=G),
-                                  src[:].bitcast(I32).rearrange("p (g h w) -> p h g w", h=NCH, g=G))
+            nc.vector.tensor_copy(dst[:].bitcast(I32).rearrange("p (h g w) -> p h g w", h=QUARTERS, g=G),
+                                  src[:].bitcast(I32).rearrange("p (g h w) -> p h g w", h=QUARTERS, g=G))
             return dst
 
+        def quantise_columns(name, raw):
+            bf = tile(name + "_bf", [P, Q, PACK], BF16)
+            nc.vector.tensor_copy(bf[:].rearrange("p (c i) t -> p c t i", i=4),
+                                  raw[:].rearrange("p t (c i) -> p c t i", i=4))
+            codes = tile(name + "_codes", [P, Q], U32)
+            scales = tile(name + "_scales", [P, Q], U8)
+            nc.vector.quantize_mx(out=codes[:].bitcast(FP8X4), scales=scales[:],
+                                  in_=bf[:].rearrange("p c t -> p (c t)"))
+            return codes, scales
+
+        offsets = tile("offsets", [P, I // 16], U16)
+        nc.sync.dma_start(offsets[:], offs)
+
+        warm_in = tile("warm_in", [P, 1], F32, tag="w1_raw0")
+        warm_out = tile("warm_out", [P, 1], F32, tag="w1_raw1")
+        nc.gpsimd.memset(warm_in[:], 1.0)
+        nc.scalar.activation(warm_out[:], warm_in[:], ACT.Abs_reciprocal_sqrt)
+
+        tab_w = load_words("tab_w", tab_words)
+        tab_sc = load_scales("tab_sc", tab_scales, nc.gpsimd)
+        w1_rows = w1.rearrange("(p s) c -> p s c", s=PACK)
+        load_cols = R // W1_LOADS
+        w1_raw = []
+        for n in range(W1_LOADS):
+            raw = tile("w1_raw%d" % n, [P, PACK, load_cols], F32)
+            nc.sync.dma_start(raw[:], w1_rows[:, :, load_cols * n:load_cols * (n + 1)])
+            w1_raw.append(raw)
+        ident = tile("ident", [P, P], F32)
+        make_identity(nc, ident[:])
+        window = tile("window", [P, T], F32)
+        nc.vector.memset(window[:], 0.0)
+
         tab_gw = gather("tab_gw", tab_w, U16)
-        keys_w = load_words("keys_w", keys_words, "words")
+        keys_w = load_words("keys_w", keys_words)
         tab_gs = gather("tab_gs", tab_sc, U8)
+        keys_sc = load_scales("keys_sc", keys_scales, nc.vector)
         tab_dw = deal("tab_dw", tab_gw, U16)
         tab_ds = deal("tab_ds", tab_gs, U8)
 
         w1_bf = tile("w1_bf", [P, PACK, P, PACK], BF16)
-        for c in range(4):
-            src = w1_raw[c // 2][:, :, 128 * (c % 2):128 * (c % 2 + 1)].rearrange("p j (m t) -> p t m j", t=PACK)
-            dst = w1_bf[:, :, 32 * c:32 * (c + 1), :]
-            if c >= 3:
+        copy_cols = R // W1_COPIES
+        copy_words = P // W1_COPIES
+        for c in range(W1_COPIES):
+            n, first = divmod(copy_cols * c, load_cols)
+            src = w1_raw[n][:, :, first:first + copy_cols].rearrange("p s (m t) -> p m s t", t=PACK)
+            dst = w1_bf[:, :, copy_words * c:copy_words * (c + 1), :].rearrange("p t m s -> p m s t")
+            if c == W1_COPIES - 1:
                 nc.vector.tensor_copy(dst, src)
             else:
                 nc.scalar.copy(dst, src)
         q_raw = tile("q_raw", [P, PACK, Q], F32, tag="w1_raw0")
-        nc.sync.dma_start(q_raw[:], query.rearrange("(p j) c -> p j c", j=PACK))
+        nc.sync.dma_start(q_raw[:], query.rearrange("(p t) c -> p t c", t=PACK))
         g_raw = tile("g_raw", [P, PACK, Q], F32, tag="w1_raw1")
-        nc.sync.dma_start(g_raw[:], gout.rearrange("(p j) c -> p j c", j=PACK))
+        nc.sync.dma_start(g_raw[:], gout.rearrange("(p t) c -> p t c", t=PACK))
         w1_codes = tile("w1_codes", [P, R], U32)
         w1_scales = tile("w1_scales", [P, R], U8)
         for t in range(PACK):
             cols = slice(P * t, P * (t + 1))
             nc.vector.quantize_mx(out=w1_codes[:, cols].bitcast(FP8X4), scales=w1_scales[:, cols],
-                                  in_=w1_bf[:, t].rearrange("p m j -> p (m j)"))
+                                  in_=w1_bf[:, t].rearrange("p m s -> p (m s)"))
 
         gain_sb = tile("gain_sb", [P, PACK], F32, tag="tab_sc")
-        nc.sync.dma_start(gain_sb[:], gain.rearrange("(p j) o -> p (j o)", j=PACK))
+        nc.sync.dma_start(gain_sb[:], gain.rearrange("(p t) o -> p (t o)", t=PACK))
         th_sb = tile("th_sb", [P, 1], F32, tag="tab_gw")
         nc.sync.dma_start(th_sb[:], th)
         hsc_sb = tile("hsc_sb", [P, PACK], F32, tag="tab_gs")
-        nc.sync.dma_start(hsc_sb[:], hsc.rearrange("(p j) o -> p (j o)", j=PACK))
+        nc.sync.dma_start(hsc_sb[:], hsc.rearrange("(p t) o -> p (t o)", t=PACK))
 
         zh = []
-        for h in range(NCH):
-            bank = ps.tile([P, PACK, CH], F32, name="zh%d" % h)
-            slots = slice(CH * h, CH * (h + 1))
+        for h in range(QUARTERS):
+            bank = ps.tile([P, PACK, BANK_SLOTS], F32, name="zh%d" % h)
+            slots = slice(BANK_SLOTS * h, BANK_SLOTS * (h + 1))
             for t in range(PACK):
                 cols = slice(P * t, P * (t + 1))
                 nc.tensor.matmul_mx(out=bank[:, t, :], lhsT=w1_codes[:, cols].bitcast(FP8X4),
@@ -123,36 +157,27 @@ def tile_attend_blrscaled_capped_kernel(tc, query, keys_words, keys_scales, th, 
                                     rhs_scale=tab_ds[:, slots], start=True, stop=True)
             zh.append(bank)
 
-        sq_pe = tile("sq_pe", [P, NCH, RUN, G * PACK], F32)
-        ssq_t = ps.tile([P, P], F32, name="ssq_t", tag="shared")
-        for h in range(NCH):
-            nc.scalar.activation(sq_pe[:, h].rearrange("p j (g t) -> p j g t", t=PACK),
+        sq = tile("sq", [P, QUARTERS, RUN, G * PACK], F32)
+        ssq_t = ps.tile([P, P], F32, name="ssq_t", tag="sums_then_scores")
+        for h in range(QUARTERS):
+            nc.scalar.activation(sq[:, h].rearrange("p j (g t) -> p j g t", t=PACK),
                                  zh[h][:].rearrange("p t (g j) -> p j g t", j=RUN), ACT.Square)
             for j in range(RUN):
-                nc.tensor.matmul(ssq_t[:], sq_pe[:, h, j, :], ident[:], is_transpose=True,
-                                 start=(h == 0 and j == 0), stop=(h == NCH - 1 and j == RUN - 1))
+                nc.tensor.matmul(ssq_t[:], sq[:, h, j, :], ident[:], is_transpose=True,
+                                 start=(h == 0 and j == 0), stop=(h == QUARTERS - 1 and j == RUN - 1))
         inv_t = tile("inv_t", [P, P], F32)
         nc.scalar.activation(inv_t[:], ssq_t[:], ACT.Abs_reciprocal_sqrt, bias=0.1, scale=1.0 / PAGE)
         inv = ps.tile([P, G, PACK], F32, name="inv")
         nc.tensor.transpose(inv[:].rearrange("p g t -> p (g t)"), inv_t[:], ident[:])
-        old_sb = tile("old_sb", [P, T], F32, tag="sq_pe")
+        old_sb = tile("old_sb", [P, T], F32, tag="sq")
         nc.sync.dma_start(old_sb[:], old)
-
-        def quantise_cols(name, raw, copy, tag):
-            bf = tile(name + "_bf", [P, Q, PACK], BF16, tag)
-            copy(bf[:].rearrange("p (c i) j -> p c j i", i=4), raw[:].rearrange("p j (c i) -> p c j i", i=4))
-            codes = tile(name + "_codes", [P, Q], U32)
-            scales = tile(name + "_scales", [P, Q], U8)
-            nc.vector.quantize_mx(out=codes[:].bitcast(FP8X4), scales=scales[:],
-                                  in_=bf[:].rearrange("p c j -> p (c j)"))
-            return codes, scales
 
         keys_gw = gather("keys_gw", keys_w, U16)
         keys_gs = gather("keys_gs", keys_sc, U8)
         res_sb = tile("res_sb", [P, 1], F32, tag="keys_sc")
         nc.sync.dma_start(res_sb[:], reserve)
-        q_codes, q_scales = quantise_cols("q", q_raw, nc.vector.tensor_copy, "q_bf")
-        score = ps.tile([P, I], F32, name="score", tag="shared")
+        q_codes, q_scales = quantise_columns("q", q_raw)
+        score = ps.tile([P, I], F32, name="score", tag="sums_then_scores")
         nc.tensor.matmul_mx(out=score[:], lhsT=q_codes[:].bitcast(FP8X4), lhsT_scale=q_scales[:],
                             rhs=keys_gw[:].bitcast(FP4X4), rhs_scale=keys_gs[:], start=True, stop=True)
         fac = tile("fac", [P, G, PACK], F32)
@@ -163,72 +188,62 @@ def tile_attend_blrscaled_capped_kernel(tc, query, keys_words, keys_scales, th, 
         nc.vector.tensor_scalar(neg_half_th[:], th_sb[:], -0.5, None, ALU.mult)
 
         c0 = ps.tile([P, I], F32, name="c0")
-        u = [tile("u%d" % h, [P, CH * PACK], F32) for h in range(NCH)]
-        hv = [tile("hv%d" % h, [P, CH, PACK], F32) for h in range(NCH)]
-        for h in range(NCH):
+        u = [tile("u%d" % h, [P, BANK_SLOTS * PACK], F32) for h in range(QUARTERS)]
+        hv = [tile("hv%d" % h, [P, BANK_SLOTS, PACK], F32) for h in range(QUARTERS)]
+        for h in range(QUARTERS):
             nc.vector.tensor_tensor(
                 u[h][:].rearrange("p (g j t) -> p g j t", j=RUN, t=PACK),
                 zh[h][:].rearrange("p t (g j) -> p g j t", j=RUN),
                 fac[:].unsqueeze(2).to_broadcast([P, G, RUN, PACK]), ALU.mult)
-        g_codes, g_scales = quantise_cols("g", g_raw, nc.vector.tensor_copy, "g_bf")
-        relu = u[2][:]
+        g_codes, g_scales = quantise_columns("g", g_raw)
+
+        relu, tanh, logs = u[2], u[3], u[1]
         sum_relu = tile("sum_relu", [P, 1], F32)
-        tanh = u[3]
-        logs = u[1]
         abs_tanh = tile("abs_tanh", [P, I], F32)
-        score_dealt = score[:].rearrange("p (g h j) -> p h g j", h=NCH, j=RUN)
-
-        def dealt(ap):
-            return ap.rearrange("p (h g j) -> p h g j", h=NCH, j=RUN)
-
-        def listed(ap):
-            return ap.rearrange("p (h g j) -> p g h j", h=NCH, j=RUN)
-
-        def by_page(ap):
-            return ap.rearrange("p (g h j) -> p g h j", h=NCH, j=RUN)
-
-        for h in range(NCH):
+        for h in range(QUARTERS):
             nc.scalar.activation(hv[h][:].rearrange("p i t -> p (i t)"), u[h][:], ACT.Silu)
-            if h == 3:
-                nc.scalar.activation(dealt(tanh[:]), score_dealt, ACT.Tanh, bias=neg_half_th[:], scale=0.5)
-        nc.scalar.activation(dealt(relu), score_dealt, ACT.Relu, bias=neg_th[:], accum_out=sum_relu[:])
-        for h in range(NCH):
-            hs = tile("hs%d" % h, [P, CH, PACK], BF16)
-            nc.vector.tensor_tensor(hs[:], hv[h][:], hsc_sb[:].unsqueeze(1).to_broadcast([P, CH, PACK]), ALU.mult)
-            codes = tile("hs_codes%d" % h, [P, CH], U32)
-            scales = tile("hs_scales%d" % h, [P, CH], U8)
+        nc.scalar.activation(as_dealt(tanh[:]), dealt_from_listed(score[:]), ACT.Tanh, bias=neg_half_th[:], scale=0.5)
+        nc.scalar.activation(as_dealt(relu[:]), dealt_from_listed(score[:]), ACT.Relu, bias=neg_th[:],
+                             accum_out=sum_relu[:])
+        for h in range(QUARTERS):
+            hs = tile("hs%d" % h, [P, BANK_SLOTS, PACK], BF16)
+            nc.vector.tensor_tensor(hs[:], hv[h][:], hsc_sb[:].unsqueeze(1).to_broadcast([P, BANK_SLOTS, PACK]),
+                                    ALU.mult)
+            codes = tile("hs_codes%d" % h, [P, BANK_SLOTS], U32)
+            scales = tile("hs_scales%d" % h, [P, BANK_SLOTS], U8)
             nc.vector.quantize_mx(out=codes[:].bitcast(FP8X4), scales=scales[:],
                                   in_=hs[:].rearrange("p i t -> p (i t)"))
-            nc.tensor.matmul_mx(out=c0[:, CH * h:CH * (h + 1)], lhsT=g_codes[:].bitcast(FP8X4),
+            nc.tensor.matmul_mx(out=c0[:, BANK_SLOTS * h:BANK_SLOTS * (h + 1)], lhsT=g_codes[:].bitcast(FP8X4),
                                 lhsT_scale=g_scales[:], rhs=codes[:].bitcast(FP8X4), rhs_scale=scales[:],
                                 start=True, stop=True)
 
         nc.vector.scalar_tensor_tensor(abs_tanh[:], tanh[:], -1.0, tanh[:], ALU.mult, ALU.max)
-        base = tile("base", [P, 1], F32)
-        nc.scalar.activation(base[:], sum_relu[:], ACT.Identity, bias=res_sb[:])
-        sum_log = tile("sum_log", [P, 1], F32)
-        nc.scalar.activation(logs[:], abs_tanh[:], ACT.Ln, bias=0.5, scale=0.5, accum_out=sum_log[:])
+        z_relu = tile("z_relu", [P, 1], F32)
+        nc.scalar.activation(z_relu[:], sum_relu[:], ACT.Identity, bias=res_sb[:])
+        sum_logs = tile("sum_logs", [P, 1], F32)
+        nc.scalar.activation(logs[:], abs_tanh[:], ACT.Ln, bias=0.5, scale=0.5, accum_out=sum_logs[:])
         z = tile("z", [P, 1], F32)
-        nc.scalar.activation(z[:], sum_log[:], ACT.Identity, bias=base[:], scale=-1.0)
+        nc.scalar.activation(z[:], sum_logs[:], ACT.Identity, bias=z_relu[:], scale=-1.0)
         sig = abs_tanh
-        nc.scalar.activation(by_page(sig[:]), listed(tanh[:]), ACT.Identity, bias=256.0, scale=256.0)
+        nc.scalar.activation(as_listed(sig[:]), listed_from_dealt(tanh[:]), ACT.Identity, bias=256.0, scale=256.0)
 
-        junk = tile("junk", [P, I], F32)
+        c0_relu = tile("c0_relu", [P, I], F32)
         dot_relu = tile("dot_relu", [P, 1], F32)
-        nc.vector.scalar_tensor_tensor(junk[:], c0[:], 1.0, relu, ALU.mult, ALU.mult, accum_out=dot_relu[:])
-        junk2 = tile("junk2", [P, I], F32)
-        dot_log = tile("dot_log", [P, 1], F32)
-        nc.vector.scalar_tensor_tensor(junk2[:], c0[:], 1.0, logs[:], ALU.mult, ALU.mult, accum_out=dot_log[:])
-        rz = tile("rz", [P, 1], F32)
-        nc.vector.reciprocal(rz[:], z[:])
+        nc.vector.scalar_tensor_tensor(c0_relu[:], c0[:], 1.0, relu[:], ALU.mult, ALU.mult, accum_out=dot_relu[:])
+        c0_logs = tile("c0_logs", [P, I], F32)
+        dot_logs = tile("dot_logs", [P, 1], F32)
+        nc.vector.scalar_tensor_tensor(c0_logs[:], c0[:], 1.0, logs[:], ALU.mult, ALU.mult, accum_out=dot_logs[:])
+        inv_z = tile("inv_z", [P, 1], F32)
+        nc.vector.reciprocal(inv_z[:], z[:])
         shift = tile("shift", [P, 1], F32)
-        nc.vector.tensor_scalar(shift[:], dot_log[:], dot_relu[:], rz[:], ALU.subtract, ALU.mult)
+        nc.vector.tensor_scalar(shift[:], dot_logs[:], dot_relu[:], inv_z[:], ALU.subtract, ALU.mult)
         dp = tile("dp", [P, I], F32)
-        nc.vector.tensor_scalar(by_page(dp[:]), listed(c0[:]), shift[:], rz[:], ALU.add, ALU.mult)
+        nc.vector.tensor_scalar(as_listed(dp[:]), listed_from_dealt(c0[:]), shift[:], inv_z[:], ALU.add, ALU.mult)
         nc.vector.tensor_tensor(window[:].indirect(offsets[:]), dp[:], sig[:], ALU.mult)
 
         for c in range(len(OUT_EDGES) - 1):
             cols = slice(OUT_EDGES[c], OUT_EDGES[c + 1])
-            res = tile("res%d" % c, [P, OUT_EDGES[c + 1] - OUT_EDGES[c]], F32)
-            nc.vector.tensor_tensor(res[:], window[:, cols], old_sb[:, cols], ALU.add)
-            (nc.sync if c % 2 == 0 else nc.scalar).dma_start(out[:, cols], res[:])
+            piece = tile("piece%d" % c, [P, OUT_EDGES[c + 1] - OUT_EDGES[c]], F32)
+            nc.vector.tensor_tensor(piece[:], window[:, cols], old_sb[:, cols], ALU.add)
+            queue = nc.sync if c % 2 == 0 else nc.scalar
+            queue.dma_start(out[:, cols], piece[:])

from contextlib import ExitStack

import concourse.mybir as mybir
from concourse.masks import make_identity

D, K, R, T, I, Q, G = 512, 512, 512, 2048, 512, 128, 32
FLOPS = 2 * I * (D * Q + K * R + R * Q)

F32 = mybir.dt.float32
BF16 = mybir.dt.bfloat16
I32 = mybir.dt.int32
U32 = mybir.dt.uint32
U16 = mybir.dt.uint16
U8 = mybir.dt.uint8
FP8X4 = mybir.dt.float8_e4m3fn_x4
FP4X4 = mybir.dt.float4_e2m1fn_x4
ACT = mybir.ActivationFunctionType
ALU = mybir.AluOpType

P = 128
PACK = 4
PAGE = I // G
QUARTERS = 4
RUN = PAGE // QUARTERS
BANK_SLOTS = G * RUN
W1_LOADS = 2
W1_COPIES = 4
OUT_EDGES = (0, 256, 768, 1280, 1792, 2048)


def dealt_from_listed(ap):
    return ap.rearrange("p (g h j) -> p h g j", h=QUARTERS, j=RUN)


def listed_from_dealt(ap):
    return ap.rearrange("p (h g j) -> p g h j", h=QUARTERS, j=RUN)


def as_dealt(ap):
    return ap.rearrange("p (h g j) -> p h g j", h=QUARTERS, j=RUN)


def as_listed(ap):
    return ap.rearrange("p (g h j) -> p g h j", h=QUARTERS, j=RUN)


def tile_attend_blrscaled_capped_kernel(tc, query, keys_words, keys_scales, th, reserve, tab_words, tab_scales,
                                         w1, gain, gout, hsc, old, offs, out):
    nc = tc.nc
    with ExitStack() as ctx:
        sb = ctx.enter_context(tc.tile_pool(name="sb", bufs=1))
        ps = ctx.enter_context(tc.psum_pool(name="ps", bufs=1))

        def tile(name, shape, dtype, tag=None):
            return sb.tile(shape, dtype, name=name, tag=tag or name, align_bytes=64)

        def load_scales(name, src, clear):
            plane = tile(name, [P, T], U8)
            clear.memset(plane[:].bitcast(I32), 0)
            for quad in range(4):
                nc.sync.dma_start(plane[32 * quad:32 * quad + 4, :].bitcast(I32),
                                  src[0, 4 * quad:4 * quad + 4, :].bitcast(I32))
            return plane

        def load_words(name, src):
            words = tile(name, [P, T], U16, "words")
            nc.sync.dma_start(words[:].bitcast(I32), src[0].bitcast(I32))
            return words

        def gather(name, src, dtype):
            dst = tile(name, [P, I], dtype)
            nc.vector.tensor_copy(dst[:], src[:].indirect(offsets[:]))
            return dst

        def deal(name, src, dtype):
            dst = tile(name, [P, I], dtype)
            nc.vector.tensor_copy(dst[:].bitcast(I32).rearrange("p (h g w) -> p h g w", h=QUARTERS, g=G),
                                  src[:].bitcast(I32).rearrange("p (g h w) -> p h g w", h=QUARTERS, g=G))
            return dst

        def quantise_columns(name, raw):
            bf = tile(name + "_bf", [P, Q, PACK], BF16)
            nc.vector.tensor_copy(bf[:].rearrange("p (c i) t -> p c t i", i=4),
                                  raw[:].rearrange("p t (c i) -> p c t i", i=4))
            codes = tile(name + "_codes", [P, Q], U32)
            scales = tile(name + "_scales", [P, Q], U8)
            nc.vector.quantize_mx(out=codes[:].bitcast(FP8X4), scales=scales[:],
                                  in_=bf[:].rearrange("p c t -> p (c t)"))
            return codes, scales

        offsets = tile("offsets", [P, I // 16], U16)
        nc.sync.dma_start(offsets[:], offs)

        warm_in = tile("warm_in", [P, 1], F32, tag="w1_raw0")
        warm_out = tile("warm_out", [P, 1], F32, tag="w1_raw1")
        nc.gpsimd.memset(warm_in[:], 1.0)
        nc.scalar.activation(warm_out[:], warm_in[:], ACT.Abs_reciprocal_sqrt)

        tab_w = load_words("tab_w", tab_words)
        tab_sc = load_scales("tab_sc", tab_scales, nc.gpsimd)
        w1_rows = w1.rearrange("(p s) c -> p s c", s=PACK)
        load_cols = R // W1_LOADS
        w1_raw = []
        for n in range(W1_LOADS):
            raw = tile("w1_raw%d" % n, [P, PACK, load_cols], F32)
            nc.sync.dma_start(raw[:], w1_rows[:, :, load_cols * n:load_cols * (n + 1)])
            w1_raw.append(raw)
        ident = tile("ident", [P, P], F32)
        make_identity(nc, ident[:])
        window = tile("window", [P, T], F32)
        nc.vector.memset(window[:], 0.0)

        tab_gw = gather("tab_gw", tab_w, U16)
        keys_w = load_words("keys_w", keys_words)
        tab_gs = gather("tab_gs", tab_sc, U8)
        keys_sc = load_scales("keys_sc", keys_scales, nc.vector)
        tab_dw = deal("tab_dw", tab_gw, U16)
        tab_ds = deal("tab_ds", tab_gs, U8)

        w1_bf = tile("w1_bf", [P, PACK, P, PACK], BF16)
        copy_cols = R // W1_COPIES
        copy_words = P // W1_COPIES
        for c in range(W1_COPIES):
            n, first = divmod(copy_cols * c, load_cols)
            src = w1_raw[n][:, :, first:first + copy_cols].rearrange("p s (m t) -> p m s t", t=PACK)
            dst = w1_bf[:, :, copy_words * c:copy_words * (c + 1), :].rearrange("p t m s -> p m s t")
            if c == W1_COPIES - 1:
                nc.vector.tensor_copy(dst, src)
            else:
                nc.scalar.copy(dst, src)
        q_raw = tile("q_raw", [P, PACK, Q], F32, tag="w1_raw0")
        nc.sync.dma_start(q_raw[:], query.rearrange("(p t) c -> p t c", t=PACK))
        g_raw = tile("g_raw", [P, PACK, Q], F32, tag="w1_raw1")
        nc.sync.dma_start(g_raw[:], gout.rearrange("(p t) c -> p t c", t=PACK))
        w1_codes = tile("w1_codes", [P, R], U32)
        w1_scales = tile("w1_scales", [P, R], U8)
        for t in range(PACK):
            cols = slice(P * t, P * (t + 1))
            nc.vector.quantize_mx(out=w1_codes[:, cols].bitcast(FP8X4), scales=w1_scales[:, cols],
                                  in_=w1_bf[:, t].rearrange("p m s -> p (m s)"))

        gain_sb = tile("gain_sb", [P, PACK], F32, tag="tab_sc")
        nc.sync.dma_start(gain_sb[:], gain.rearrange("(p t) o -> p (t o)", t=PACK))
        th_sb = tile("th_sb", [P, 1], F32, tag="tab_gw")
        nc.sync.dma_start(th_sb[:], th)
        hsc_sb = tile("hsc_sb", [P, PACK], F32, tag="tab_gs")
        nc.sync.dma_start(hsc_sb[:], hsc.rearrange("(p t) o -> p (t o)", t=PACK))

        zh = []
        for h in range(QUARTERS):
            bank = ps.tile([P, PACK, BANK_SLOTS], F32, name="zh%d" % h)
            slots = slice(BANK_SLOTS * h, BANK_SLOTS * (h + 1))
            for t in range(PACK):
                cols = slice(P * t, P * (t + 1))
                nc.tensor.matmul_mx(out=bank[:, t, :], lhsT=w1_codes[:, cols].bitcast(FP8X4),
                                    lhsT_scale=w1_scales[:, cols], rhs=tab_dw[:, slots].bitcast(FP4X4),
                                    rhs_scale=tab_ds[:, slots], start=True, stop=True)
            zh.append(bank)

        sq = tile("sq", [P, QUARTERS, RUN, G * PACK], F32)
        ssq_t = ps.tile([P, P], F32, name="ssq_t", tag="sums_then_scores")
        for h in range(QUARTERS):
            nc.scalar.activation(sq[:, h].rearrange("p j (g t) -> p j g t", t=PACK),
                                 zh[h][:].rearrange("p t (g j) -> p j g t", j=RUN), ACT.Square)
            for j in range(RUN):
                nc.tensor.matmul(ssq_t[:], sq[:, h, j, :], ident[:], is_transpose=True,
                                 start=(h == 0 and j == 0), stop=(h == QUARTERS - 1 and j == RUN - 1))
        inv_t = tile("inv_t", [P, P], F32)
        nc.scalar.activation(inv_t[:], ssq_t[:], ACT.Abs_reciprocal_sqrt, bias=0.1, scale=1.0 / PAGE)
        inv = ps.tile([P, G, PACK], F32, name="inv")
        nc.tensor.transpose(inv[:].rearrange("p g t -> p (g t)"), inv_t[:], ident[:])
        old_sb = tile("old_sb", [P, T], F32, tag="sq")
        nc.sync.dma_start(old_sb[:], old)

        keys_gw = gather("keys_gw", keys_w, U16)
        keys_gs = gather("keys_gs", keys_sc, U8)
        res_sb = tile("res_sb", [P, 1], F32, tag="keys_sc")
        nc.sync.dma_start(res_sb[:], reserve)
        q_codes, q_scales = quantise_columns("q", q_raw)
        score = ps.tile([P, I], F32, name="score", tag="sums_then_scores")
        nc.tensor.matmul_mx(out=score[:], lhsT=q_codes[:].bitcast(FP8X4), lhsT_scale=q_scales[:],
                            rhs=keys_gw[:].bitcast(FP4X4), rhs_scale=keys_gs[:], start=True, stop=True)
        fac = tile("fac", [P, G, PACK], F32)
        nc.vector.tensor_tensor(fac[:], inv[:], gain_sb[:].unsqueeze(1).to_broadcast([P, G, PACK]), ALU.mult)
        neg_th = tile("neg_th", [P, 1], F32)
        nc.vector.tensor_scalar(neg_th[:], th_sb[:], -1.0, None, ALU.mult)
        neg_half_th = tile("neg_half_th", [P, 1], F32)
        nc.vector.tensor_scalar(neg_half_th[:], th_sb[:], -0.5, None, ALU.mult)

        c0 = ps.tile([P, I], F32, name="c0")
        u = [tile("u%d" % h, [P, BANK_SLOTS * PACK], F32) for h in range(QUARTERS)]
        hv = [tile("hv%d" % h, [P, BANK_SLOTS, PACK], F32) for h in range(QUARTERS)]
        for h in range(QUARTERS):
            nc.vector.tensor_tensor(
                u[h][:].rearrange("p (g j t) -> p g j t", j=RUN, t=PACK),
                zh[h][:].rearrange("p t (g j) -> p g j t", j=RUN),
                fac[:].unsqueeze(2).to_broadcast([P, G, RUN, PACK]), ALU.mult)
        g_codes, g_scales = quantise_columns("g", g_raw)

        relu, tanh, logs = u[2], u[3], u[1]
        sum_relu = tile("sum_relu", [P, 1], F32)
        abs_tanh = tile("abs_tanh", [P, I], F32)
        for h in range(QUARTERS):
            nc.scalar.activation(hv[h][:].rearrange("p i t -> p (i t)"), u[h][:], ACT.Silu)
        nc.scalar.activation(as_dealt(tanh[:]), dealt_from_listed(score[:]), ACT.Tanh, bias=neg_half_th[:], scale=0.5)
        nc.scalar.activation(as_dealt(relu[:]), dealt_from_listed(score[:]), ACT.Relu, bias=neg_th[:],
                             accum_out=sum_relu[:])
        for h in range(QUARTERS):
            hs = tile("hs%d" % h, [P, BANK_SLOTS, PACK], BF16)
            nc.vector.tensor_tensor(hs[:], hv[h][:], hsc_sb[:].unsqueeze(1).to_broadcast([P, BANK_SLOTS, PACK]),
                                    ALU.mult)
            codes = tile("hs_codes%d" % h, [P, BANK_SLOTS], U32)
            scales = tile("hs_scales%d" % h, [P, BANK_SLOTS], U8)
            nc.vector.quantize_mx(out=codes[:].bitcast(FP8X4), scales=scales[:],
                                  in_=hs[:].rearrange("p i t -> p (i t)"))
            nc.tensor.matmul_mx(out=c0[:, BANK_SLOTS * h:BANK_SLOTS * (h + 1)], lhsT=g_codes[:].bitcast(FP8X4),
                                lhsT_scale=g_scales[:], rhs=codes[:].bitcast(FP8X4), rhs_scale=scales[:],
                                start=True, stop=True)

        nc.vector.scalar_tensor_tensor(abs_tanh[:], tanh[:], -1.0, tanh[:], ALU.mult, ALU.max)
        z_relu = tile("z_relu", [P, 1], F32)
        nc.scalar.activation(z_relu[:], sum_relu[:], ACT.Identity, bias=res_sb[:])
        sum_logs = tile("sum_logs", [P, 1], F32)
        nc.scalar.activation(logs[:], abs_tanh[:], ACT.Ln, bias=0.5, scale=0.5, accum_out=sum_logs[:])
        z = tile("z", [P, 1], F32)
        nc.scalar.activation(z[:], sum_logs[:], ACT.Identity, bias=z_relu[:], scale=-1.0)
        sig = abs_tanh
        nc.scalar.activation(as_listed(sig[:]), listed_from_dealt(tanh[:]), ACT.Identity, bias=256.0, scale=256.0)

        c0_relu = tile("c0_relu", [P, I], F32)
        dot_relu = tile("dot_relu", [P, 1], F32)
        nc.vector.scalar_tensor_tensor(c0_relu[:], c0[:], 1.0, relu[:], ALU.mult, ALU.mult, accum_out=dot_relu[:])
        c0_logs = tile("c0_logs", [P, I], F32)
        dot_logs = tile("dot_logs", [P, 1], F32)
        nc.vector.scalar_tensor_tensor(c0_logs[:], c0[:], 1.0, logs[:], ALU.mult, ALU.mult, accum_out=dot_logs[:])
        inv_z = tile("inv_z", [P, 1], F32)
        nc.vector.reciprocal(inv_z[:], z[:])
        shift = tile("shift", [P, 1], F32)
        nc.vector.tensor_scalar(shift[:], dot_logs[:], dot_relu[:], inv_z[:], ALU.subtract, ALU.mult)
        dp = tile("dp", [P, I], F32)
        nc.vector.tensor_scalar(as_listed(dp[:]), listed_from_dealt(c0[:]), shift[:], inv_z[:], ALU.add, ALU.mult)
        nc.vector.tensor_tensor(window[:].indirect(offsets[:]), dp[:], sig[:], ALU.mult)

        for c in range(len(OUT_EDGES) - 1):
            cols = slice(OUT_EDGES[c], OUT_EDGES[c + 1])
            piece = tile("piece%d" % c, [P, OUT_EDGES[c + 1] - OUT_EDGES[c]], F32)
            nc.vector.tensor_tensor(piece[:], window[:, cols], old_sb[:, cols], ALU.add)
            queue = nc.sync if c % 2 == 0 else nc.scalar
            queue.dma_start(out[:, cols], piece[:])
